import numpy as np
import ml_dtypes


def mxq(x, axis, fmt="e4m3"):
    dtype, down = {"e4m3": (ml_dtypes.float8_e4m3fn, 7), "e5m2": (ml_dtypes.float8_e5m2, 14)}[fmt]
    v = np.moveaxis(np.asarray(x, np.float32).astype(ml_dtypes.bfloat16).astype(np.float64), axis, -1)
    blocks = v.reshape(v.shape[:-1] + (-1, 32))
    amax = np.abs(blocks).max(-1, keepdims=True)
    byte = np.maximum(np.where(amax > 0, np.frexp(amax)[1] - 1 + 127, 0) - down, 1)
    scale = np.exp2(byte - 127.0)
    codes = (blocks / scale).astype(np.float32).astype(dtype).astype(np.float64)
    return np.moveaxis((codes * scale).reshape(v.shape), -1, axis)


WIDE = False


def mx_kscale(k):
    if not WIDE:
        return np.ones(k)
    levels = np.array([10, -10, 5, -5, 0])
    if k % 512:
        return np.exp2(np.random.permutation(np.resize(levels, k // 32))).repeat(32)
    a = np.empty((k // 512, 16))
    for p in range(k // 512):
        a[p, :8] = np.random.permutation(np.resize(levels, 8))
        for g in range(8):
            far = levels[np.abs(levels - a[p, g]) >= 10]
            a[p, g + 8] = far[np.random.randint(len(far))]
    return np.exp2(a.ravel()).repeat(32)


def f64(x):
    return np.asarray(x).astype(np.float64)


def striped(idx):
    return np.tile(idx.reshape(-1, 16).T, (8, 1)).astype(np.uint16)


def unstriped(offs):
    return offs[:16].T.reshape(-1).astype(np.int64)


def striped8(idx):
    return np.concatenate([x.reshape(-1, 16).T for x in idx]).astype(np.uint16)


def runs(offs, k):
    lists = np.stack([offs[16 * r : 16 * r + 16].T.reshape(-1) for r in range(8)]).astype(np.int64)
    return lists[np.arange(k) % 512 // 64]


def pack_weight(w):
    k, n = w.shape
    w = f64(np.asarray(w, np.float32).astype(ml_dtypes.bfloat16)).reshape(k // 32, 32, n)
    amax = np.abs(w).max(1)
    byte = np.clip(np.where(amax > 0, np.frexp(amax)[1] - 1 + 127 - 7, 1), 1, 254)
    scaled = (w * np.exp2(127.0 - byte)[:, None, :]).reshape(k, n).astype(np.float32)
    words = np.ascontiguousarray(scaled.reshape(k // 512, 128, 4, n).transpose(0, 1, 3, 2)).astype(ml_dtypes.float8_e4m3fn).view(np.uint8)
    return words, np.ascontiguousarray(byte.astype(np.uint8).reshape(k // 512, 16, n))


def unpack_weight(words, scales):
    g, p, n, _ = words.shape
    vals = np.ascontiguousarray(words).view(ml_dtypes.float8_e4m3fn).astype(np.float64) * np.repeat(np.exp2(scales.astype(np.float64) - 127.0), 8, axis=1)[..., None]
    return vals.transpose(0, 1, 3, 2).reshape(g * 512, n)


def sigmoid(v):
    return 1.0 / (1.0 + np.exp(-np.maximum(v, -700.0)))

def planes(y):
    n, m = y.shape
    v = y.astype(np.float32).astype(ml_dtypes.bfloat16).astype(np.float64).reshape(n // 32, 32, m)
    top = np.abs(v).max(1)
    byte = np.clip(np.where(top > 0, np.frexp(top)[1] - 1 + 127 - 7, 1), 1, 254)
    codes = (v * np.exp2(127.0 - byte)[:, None, :]).reshape(n, m).astype(np.float32).astype(ml_dtypes.float8_e4m3fn).view(np.uint8)
    words = codes.reshape(n // 512, 128, 4, m).transpose(0, 1, 3, 2)
    return np.ascontiguousarray(words), np.ascontiguousarray(byte.astype(np.uint8).reshape(n // 512, 16, m))


K, T, S, N, H, G = 512, 2048, 512, 512, 512, 2048


def setup_inputs():
    n = np.random.standard_normal
    s = mx_kscale(K)[:, None]
    u = mx_kscale(S)
    packed_xT = pack_weight(n((K, T)) * s)
    packed_w1 = pack_weight(n((K, H)) / np.sqrt(K) / s)
    packed_w2 = pack_weight(n((H, N)) / np.sqrt(H) / u[:, None])
    packed_dT = pack_weight(n((K, G)) / s)
    return {
        "x_words": packed_xT[0],
        "x_scales": packed_xT[1],
        "w1_words": packed_w1[0],
        "w1_scales": packed_w1[1],
        "gn": (np.random.uniform(0.5, 1.5, (H, 1)) * u[:, None]).astype(np.float32),
        "w2_words": packed_w2[0],
        "w2_scales": packed_w2[1],
        "d_words": packed_dT[0],
        "d_scales": packed_dT[1],
        "offs": striped(np.random.permutation(T)[:S]),
        "n1": striped8(np.stack([np.random.permutation(S) for _ in range(8)])),
        "n2": striped8(np.stack([np.random.permutation(S) for _ in range(8)])),
        "two": striped(np.random.permutation(T)[:S]),
        "k1": striped8(np.random.randint(0, G, (8, H))),
        "n3": striped(np.random.permutation(S)),
        "n4": striped(np.random.permutation(S)),
    }


def reference(x_words, x_scales, w1_words, w1_scales, gn, w2_words, w2_scales, d_words, d_scales, offs, n1, n2, two, k1, n3, n4):
    xq = unpack_weight(x_words, x_scales)[:, unstriped(offs)]
    y = unpack_weight(w1_words, w1_scales).T @ xq
    pa = y[np.arange(H)[:, None], runs(n1, H)]
    pb = y[np.arange(H)[:, None], runs(n2, H)]
    z = f64(gn) * (np.maximum(np.maximum(y, pa), pb) - (0.5 * (np.minimum(np.minimum(y, pa), pb))))
    a = unpack_weight(w2_words, w2_scales).T @ mxq(z, 0, "e4m3")
    d_k1 = unpack_weight(d_words, d_scales)[np.arange(K)[:, None], runs(k1, K)]
    x_two = unpack_weight(x_words, x_scales)[:, unstriped(two)]
    b = 0.0625 * (d_k1.T @ x_two)
    out_0 = a * (sigmoid(b[:, unstriped(n4)])) - (0.5 * a[:, unstriped(n3)])
    return (out_0,) + planes(out_0)

@@ -1,0 +1,234 @@
+from contextlib import ExitStack
+
+import concourse.mybir as mybir
+
+F32 = mybir.dt.float32
+BF16 = mybir.dt.bfloat16
+I32 = mybir.dt.int32
+U32 = mybir.dt.uint32
+U16 = mybir.dt.uint16
+U8 = mybir.dt.uint8
+FP8X4 = mybir.dt.float8_e4m3fn_x4
+ALU = mybir.AluOpType
+ACT = mybir.ActivationFunctionType
+
+P = 128
+PACK = 4
+TABLE = 2048
+S = 512
+HALF = 256
+LIST_COLS = S // 16
+HALF_COLS = HALF // 16
+
+FLOPS = 3 * 2 * 512 * 512 * 512
+
+
+def words_of(dram):
+    return dram[0].rearrange("p n t -> p (n t)").bitcast(I32)
+
+
+def deal_words(tile):
+    return tile[:].rearrange("p (b i t) -> p b t i", i=4, t=PACK)
+
+
+def dealt_words(tile):
+    return tile[:].rearrange("p (t b i) -> p b t i", i=4, t=PACK)
+
+
+def deal_scales(tile):
+    return tile[:].rearrange("p (b i t) -> p b t i", i=16, t=PACK)
+
+
+def dealt_scales(tile):
+    return tile[:].rearrange("p (t b i) -> p b t i", i=16, t=PACK)
+
+
+def by_pairs(tile):
+    return tile.rearrange("p t (c i) -> p c t i", i=2)
+
+
+def woven(tile):
+    return tile[:].rearrange("p (c i t) -> p c t i", i=2, t=PACK)
+
+
+def tile_picked_cdjoingatebrange_none_po_kernel(
+    tc, x_words, x_scales, w1_words, w1_scales, gn, w2_words, w2_scales, d_words, d_scales,
+    offs, n1, n2, two, k1, n3, n4, out_0, out_1, out_2,
+):
+    nc = tc.nc
+    with ExitStack() as ctx:
+        sb = ctx.enter_context(tc.tile_pool(name="sb", bufs=1))
+        ps = ctx.enter_context(tc.psum_pool(name="ps", bufs=1))
+
+        def new(name, shape, dtype):
+            return sb.tile(shape, dtype, name=name, align_bytes=64)
+
+        def load_list(name, dram):
+            tile = new(name, [P, LIST_COLS], U16)
+            nc.sync.dma_start(tile[:], dram)
+            return tile
+
+        def load_words(name, dram, width):
+            tile = new(name, [P, width], U32)
+            nc.sync.dma_start(out=tile[:].bitcast(I32), in_=words_of(dram))
+            return tile
+
+        def load_plane(tile, dram, quadrants):
+            for q in quadrants:
+                nc.sync.dma_start(out=tile[32 * q : 32 * q + 4, :].bitcast(I32), in_=dram[0, 4 * q : 4 * q + 4, :].bitcast(I32))
+
+        xs_table = new("xs_table", [P, TABLE], U8)
+        w1s_raw = new("w1s_raw", [P, S], U8)
+        ds_table = new("ds_table", [P, TABLE], U8)
+        w2s_raw = new("w2s_raw", [P, S], U8)
+        ds_plane = new("ds_plane", [P, S], U8)
+        nc.gpsimd.memset(w1s_raw[:].bitcast(I32), 0)
+        nc.gpsimd.memset(xs_table[:, : TABLE // 2].bitcast(I32), 0)
+        nc.vector.memset(xs_table[:, TABLE // 2 :].bitcast(I32), 0)
+        nc.vector.memset(ds_table[:].bitcast(I32), 0)
+        nc.gpsimd.memset(w2s_raw[:].bitcast(I32), 0)
+        nc.gpsimd.memset(ds_plane[:].bitcast(I32), 0)
+
+        offs_t = load_list("offs_t", offs)
+        gain = new("gain", [P, PACK], F32)
+        nc.sync.dma_start(out=gain[:], in_=gn.rearrange("(p t) o -> p (t o)", t=PACK))
+        w1w_raw = load_words("w1w_raw", w1_words, S)
+        two_t = load_list("two_t", two)
+        load_plane(w1s_raw, w1_scales, range(1))
+        xw_table = load_words("xw_table", x_words, TABLE)
+        load_plane(xs_table, x_scales, range(4))
+        load_plane(w1s_raw, w1_scales, range(1, 4))
+        k1_t = load_list("k1_t", k1)
+        for r in range(2):
+            nc.sync.dma_start(out=ds_table[r:P:16, :].bitcast(I32), in_=d_scales[0, r:16:2, :].bitcast(I32))
+        n1_t = load_list("n1_t", n1)
+        n2_t = load_list("n2_t", n2)
+        w2w_raw = load_words("w2w_raw", w2_words, S)
+        dw_table = load_words("dw_table", d_words, TABLE)
+        load_plane(w2s_raw, w2_scales, range(4))
+        n4_t = load_list("n4_t", n4)
+        n3_t = load_list("n3_t", n3)
+
+        def matmul(out, lhs_w, lhs_s, t, rhs_w, rhs_s):
+            rows = slice(P * t, P * (t + 1))
+            nc.tensor.matmul_mx(
+                out=out, lhsT=lhs_w[:, rows].bitcast(FP8X4), lhsT_scale=lhs_s[:, rows],
+                rhs=rhs_w[:].bitcast(FP8X4), rhs_scale=rhs_s[:], start=True, stop=True,
+            )
+
+        xq_s = new("xq_s", [P, S], U8)
+        xq_w = new("xq_w", [P, S], U32)
+        w1w = new("w1w", [P, S], U32)
+        w1s = new("w1s", [P, S], U8)
+        nc.vector.tensor_copy(xq_s[:], xs_table[:].indirect(offs_t[:]))
+        nc.vector.tensor_copy(xq_w[:], xw_table[:].indirect(offs_t[:]))
+        nc.scalar.copy(dealt_words(w1w), deal_words(w1w_raw))
+        nc.vector.tensor_copy(dealt_scales(w1s), deal_scales(w1s_raw))
+
+        twice = new("twice", [P, PACK], F32)
+        sign = new("sign", [P, PACK], BF16)
+        size = new("size", [P, PACK], F32)
+        nc.vector.tensor_scalar(twice[:], gain[:], 0.0, 2.0, ALU.is_ge, ALU.mult)
+        nc.scalar.activation(size[:], gain[:], ACT.Abs)
+        nc.vector.tensor_scalar(sign[:], twice[:], -1.0, None, ALU.add)
+
+        y = []
+        for t in range(PACK):
+            bank = ps.tile([P, S], F32, name="ya%d" % t, tag="ya%d" % t)
+            matmul(bank[:], w1w, w1s, t, xq_w, xq_s)
+            y.append(new("y%d" % t, [P, 2 * S], F32))
+            nc.scalar.activation(y[t][:, :S], bank[:], ACT.Copy, scale=size[:, t : t + 1])
+
+        w2w = new("w2w", [P, S], U32)
+        w2s = new("w2s", [P, S], U8)
+        nc.scalar.copy(dealt_words(w2w), deal_words(w2w_raw))
+
+        x2_s = new("x2_s", [P, S], U8)
+        x2_w = new("x2_w", [P, S], U32)
+        dq_s = new("dq_s", [P, S], U8)
+        dq_w = new("dq_w", [P, S], U32)
+        ds_dealt = new("ds_dealt", [P, S], U8)
+        dw = new("dw", [P, S], U32)
+        nc.vector.tensor_copy(dq_s[:], ds_table[:].indirect(k1_t[:]))
+        nc.vector.tensor_copy(x2_s[:], xs_table[:].indirect(two_t[:]))
+        nc.vector.tensor_copy(dealt_scales(ds_dealt), deal_scales(dq_s))
+        for r in range(4):
+            src = 16 * (r // 2) + r % 2
+            nc.sync.dma_start(out=ds_plane[r:P:32, :].bitcast(I32), in_=ds_dealt[src:P:32, :].bitcast(I32))
+        nc.vector.tensor_copy(x2_w[:], xw_table[:].indirect(two_t[:]))
+        nc.vector.tensor_copy(dq_w[:], dw_table[:].indirect(k1_t[:]))
+        nc.vector.tensor_copy(dealt_scales(w2s), deal_scales(w2s_raw))
+        nc.vector.tensor_copy(dealt_words(dw), deal_words(dq_w))
+        b_banks = []
+        for t in range(PACK):
+            b_banks.append(ps.tile([P, S], F32, name="b%d" % t))
+            matmul(b_banks[t][:], dw, ds_plane, t, x2_w, x2_s)
+
+        top = new("top", [P, PACK, S], F32)
+        low = new("low", [P, PACK, S], F32)
+        for t in range(PACK):
+            pa = new("pa%d" % t, [P, S], F32)
+            pbh = new("pbh%d" % t, [P, S], F32)
+            hi = new("hi%d" % t, [P, S], F32)
+            lo = new("lo%d" % t, [P, S], F32)
+            nc.scalar.activation(pa[:], y[t][:].indirect(n1_t[:]), ACT.Copy)
+            if t < PACK - 1:
+                nc.scalar.activation(pbh[:], y[t][:].indirect(n2_t[:]), ACT.Copy, scale=0.5)
+            else:
+                nc.vector.tensor_scalar(pbh[:], y[t][:].indirect(n2_t[:]), 0.5, 0.0, ALU.mult, ALU.add)
+            nc.vector.tensor_tensor(hi[:], y[t][:, :S], pa[:], ALU.max)
+            nc.vector.tensor_tensor(lo[:], y[t][:, :S], pa[:], ALU.min)
+            nc.vector.scalar_tensor_tensor(top[:, t, :], pbh[:], 2.0, hi[:], ALU.mult, ALU.max)
+            nc.vector.scalar_tensor_tensor(low[:, t, :], lo[:], 0.5, pbh[:], ALU.mult, ALU.min)
+
+        a_banks = [ps.tile([P, S], F32, name="a%d" % t, tag="ya%d" % t) for t in range(PACK)]
+        for h in range(2):
+            cols = slice(HALF * h, HALF * (h + 1))
+            z_abs = new("z_abs%d" % h, [P, HALF * PACK], BF16)
+            z = new("z%d" % h, [P, HALF * PACK], BF16)
+            z_w = new("z_w%d" % h, [P, HALF], U32)
+            z_s = new("z_s%d" % h, [P, HALF], U8)
+            nc.vector.tensor_tensor(woven(z_abs), by_pairs(top[:, :, cols]), by_pairs(low[:, :, cols]), ALU.subtract)
+            nc.vector.tensor_tensor(
+                z[:].rearrange("p (c t) -> p c t", t=PACK), z_abs[:].rearrange("p (c t) -> p c t", t=PACK),
+                sign[:].unsqueeze(1).to_broadcast([P, HALF, PACK]), ALU.mult,
+            )
+            nc.vector.quantize_mx(out=z_w[:].bitcast(FP8X4), scales=z_s[:], in_=z[:])
+            for t in range(PACK):
+                matmul(a_banks[t][:, cols], w2w, w2s, t, z_w, z_s)
+
+        gate = []
+        for t in range(PACK):
+            sig = new("sig%d" % t, [P, S + 16], F32)
+            nc.scalar.activation(sig[:, :S], b_banks[t][:], ACT.Tanh, scale=0.03125)
+            gate.append(new("gate%d" % t, [P, S], F32))
+            nc.scalar.activation(gate[t][:], sig[:].indirect(n4_t[:]), ACT.Copy)
+
+        a_half = [new("a_half%d" % t, [P, S], F32) for t in range(PACK)]
+        gated = [new("gated%d" % t, [P, S], F32) for t in range(PACK)]
+        for t in range(PACK):
+            nc.scalar.activation(a_half[t][:], a_banks[t][:], ACT.Copy, scale=-0.5)
+            nc.vector.scalar_tensor_tensor(gated[t][:], gate[t][:], 1.0, a_half[t][:], ALU.add, ALU.mult)
+
+        out_rows = out_0.rearrange("(p t) j -> p t j", t=PACK)
+        out_w = new("out_w", [P, S], U32)
+        out_s = new("out_s", [P, S], U8)
+        for h in range(2):
+            cols = slice(HALF * h, HALF * (h + 1))
+            lcols = slice(HALF_COLS * h, HALF_COLS * (h + 1))
+            res = new("res%d" % h, [P, PACK, HALF], F32)
+            for t in range(PACK):
+                looked_up = a_half[t][:].indirect(n3_t[:, lcols])
+                if t == 0:
+                    nc.vector.tensor_tensor(res[:, t, :], looked_up, gated[t][:, cols], ALU.subtract)
+                else:
+                    far = new("far%d%d" % (h, t), [P, HALF], F32)
+                    nc.scalar.activation(far[:], looked_up, ACT.Copy)
+                    nc.vector.tensor_tensor(res[:, t, :], far[:], gated[t][:, cols], ALU.subtract)
+            nc.sync.dma_start(out=out_rows[:, :, cols], in_=res[:])
+            res_bf = new("res_bf%d" % h, [P, HALF * PACK], BF16)
+            nc.vector.tensor_copy(woven(res_bf), by_pairs(res[:]))
+            nc.vector.quantize_mx(out=out_w[:, cols].bitcast(FP8X4), scales=out_s[:, cols], in_=res_bf[:])
+            nc.sync.dma_start(out=words_of(out_1)[:, cols], in_=out_w[:, cols].bitcast(I32))
+        for q in range(4):
+            nc.sync.dma_start(out=out_2[0, 4 * q : 4 * q + 4, :].bitcast(I32), in_=out_s[32 * q : 32 * q + 4, :].bitcast(I32))

@@ -60,8 +60,8 @@ def tile_picked_cdjoingatebrange_none_po_kernel(
         sb = ctx.enter_context(tc.tile_pool(name="sb", bufs=1))
         ps = ctx.enter_context(tc.psum_pool(name="ps", bufs=1))
 
-        def new(name, shape, dtype):
-            return sb.tile(shape, dtype, name=name, align_bytes=64)
+        def new(name, shape, dtype, over=None):
+            return sb.tile(shape, dtype, name=name, tag=over or name, align_bytes=64)
 
         def load_list(name, dram):
             tile = new(name, [P, LIST_COLS], U16)
@@ -82,29 +82,27 @@ def tile_picked_cdjoingatebrange_none_po_kernel(
         ds_table = new("ds_table", [P, TABLE], U8)
         w2s_raw = new("w2s_raw", [P, S], U8)
         ds_plane = new("ds_plane", [P, S], U8)
+        nc.gpsimd.memset(xs_table[:].bitcast(I32), 0)
         nc.gpsimd.memset(w1s_raw[:].bitcast(I32), 0)
-        nc.gpsimd.memset(xs_table[:, : TABLE // 2].bitcast(I32), 0)
-        nc.vector.memset(xs_table[:, TABLE // 2 :].bitcast(I32), 0)
         nc.vector.memset(ds_table[:].bitcast(I32), 0)
         nc.gpsimd.memset(w2s_raw[:].bitcast(I32), 0)
         nc.gpsimd.memset(ds_plane[:].bitcast(I32), 0)
 
         offs_t = load_list("offs_t", offs)
+        load_plane(xs_table, x_scales, range(4))
+        two_t = load_list("two_t", two)
+        xw_table = load_words("xw_table", x_words, TABLE)
+        w1w_raw = load_words("w1w_raw", w1_words, S)
+        load_plane(w1s_raw, w1_scales, range(4))
         gain = new("gain", [P, PACK], F32)
         nc.sync.dma_start(out=gain[:], in_=gn.rearrange("(p t) o -> p (t o)", t=PACK))
-        w1w_raw = load_words("w1w_raw", w1_words, S)
-        two_t = load_list("two_t", two)
-        load_plane(w1s_raw, w1_scales, range(1))
-        xw_table = load_words("xw_table", x_words, TABLE)
-        load_plane(xs_table, x_scales, range(4))
-        load_plane(w1s_raw, w1_scales, range(1, 4))
+        dw_table = load_words("dw_table", d_words, TABLE)
         k1_t = load_list("k1_t", k1)
         for r in range(2):
             nc.sync.dma_start(out=ds_table[r:P:16, :].bitcast(I32), in_=d_scales[0, r:16:2, :].bitcast(I32))
         n1_t = load_list("n1_t", n1)
         n2_t = load_list("n2_t", n2)
         w2w_raw = load_words("w2w_raw", w2_words, S)
-        dw_table = load_words("dw_table", d_words, TABLE)
         load_plane(w2s_raw, w2_scales, range(4))
         n4_t = load_list("n4_t", n4)
         n3_t = load_list("n3_t", n3)
@@ -141,24 +139,22 @@ def tile_picked_cdjoingatebrange_none_po_kernel(
 
         w2w = new("w2w", [P, S], U32)
         w2s = new("w2s", [P, S], U8)
-        nc.scalar.copy(dealt_words(w2w), deal_words(w2w_raw))
 
         x2_s = new("x2_s", [P, S], U8)
-        x2_w = new("x2_w", [P, S], U32)
+        x2_w = new("x2_w", [P, S], U32, over="w1s_raw")
         dq_s = new("dq_s", [P, S], U8)
         dq_w = new("dq_w", [P, S], U32)
         ds_dealt = new("ds_dealt", [P, S], U8)
         dw = new("dw", [P, S], U32)
-        nc.vector.tensor_copy(dq_s[:], ds_table[:].indirect(k1_t[:]))
         nc.vector.tensor_copy(x2_s[:], xs_table[:].indirect(two_t[:]))
+        nc.vector.tensor_copy(x2_w[:], xw_table[:].indirect(two_t[:]))
+        nc.vector.tensor_copy(dq_w[:], dw_table[:].indirect(k1_t[:]))
+        nc.vector.tensor_copy(dq_s[:], ds_table[:].indirect(k1_t[:]))
+        nc.vector.tensor_copy(dealt_words(dw), deal_words(dq_w))
         nc.vector.tensor_copy(dealt_scales(ds_dealt), deal_scales(dq_s))
         for r in range(4):
             src = 16 * (r // 2) + r % 2
             nc.sync.dma_start(out=ds_plane[r:P:32, :].bitcast(I32), in_=ds_dealt[src:P:32, :].bitcast(I32))
-        nc.vector.tensor_copy(x2_w[:], xw_table[:].indirect(two_t[:]))
-        nc.vector.tensor_copy(dq_w[:], dw_table[:].indirect(k1_t[:]))
-        nc.vector.tensor_copy(dealt_scales(w2s), deal_scales(w2s_raw))
-        nc.vector.tensor_copy(dealt_words(dw), deal_words(dq_w))
         b_banks = []
         for t in range(PACK):
             b_banks.append(ps.tile([P, S], F32, name="b%d" % t))
@@ -169,19 +165,18 @@ def tile_picked_cdjoingatebrange_none_po_kernel(
         for t in range(PACK):
             pa = new("pa%d" % t, [P, S], F32)
             pbh = new("pbh%d" % t, [P, S], F32)
-            hi = new("hi%d" % t, [P, S], F32)
-            lo = new("lo%d" % t, [P, S], F32)
+            hi = new("hi%d" % t, [P, S], F32, over=["dw_table", "dq_w", "pa0", "pa1"][t])[:]
+            lo = new("lo%d" % t, [P, S], F32, over=["ds_table", "dq_s", "pbh0", "pbh1"][t])[:]
             nc.scalar.activation(pa[:], y[t][:].indirect(n1_t[:]), ACT.Copy)
-            if t < PACK - 1:
-                nc.scalar.activation(pbh[:], y[t][:].indirect(n2_t[:]), ACT.Copy, scale=0.5)
-            else:
-                nc.vector.tensor_scalar(pbh[:], y[t][:].indirect(n2_t[:]), 0.5, 0.0, ALU.mult, ALU.add)
-            nc.vector.tensor_tensor(hi[:], y[t][:, :S], pa[:], ALU.max)
-            nc.vector.tensor_tensor(lo[:], y[t][:, :S], pa[:], ALU.min)
-            nc.vector.scalar_tensor_tensor(top[:, t, :], pbh[:], 2.0, hi[:], ALU.mult, ALU.max)
-            nc.vector.scalar_tensor_tensor(low[:, t, :], lo[:], 0.5, pbh[:], ALU.mult, ALU.min)
+            nc.scalar.activation(pbh[:], y[t][:].indirect(n2_t[:]), ACT.Copy, scale=0.5)
+            nc.vector.tensor_tensor(hi, y[t][:, :S], pa[:], ALU.max)
+            nc.vector.tensor_tensor(lo, y[t][:, :S], pa[:], ALU.min)
+            nc.vector.scalar_tensor_tensor(top[:, t, :], pbh[:], 2.0, hi, ALU.mult, ALU.max)
+            nc.vector.scalar_tensor_tensor(low[:, t, :], lo, 0.5, pbh[:], ALU.mult, ALU.min)
 
-        a_banks = [ps.tile([P, S], F32, name="a%d" % t, tag="ya%d" % t) for t in range(PACK)]
+        nc.vector.tensor_copy(dealt_words(w2w), deal_words(w2w_raw))
+        nc.vector.tensor_copy(dealt_scales(w2s), deal_scales(w2s_raw))
+        a_banks = [ps.tile([P, 2, HALF], F32, name="a%d" % n, tag="ya%d" % n) for n in range(PACK)]
         for h in range(2):
             cols = slice(HALF * h, HALF * (h + 1))
             z_abs = new("z_abs%d" % h, [P, HALF * PACK], BF16)
@@ -195,40 +190,48 @@ def tile_picked_cdjoingatebrange_none_po_kernel(
             )
             nc.vector.quantize_mx(out=z_w[:].bitcast(FP8X4), scales=z_s[:], in_=z[:])
             for t in range(PACK):
-                matmul(a_banks[t][:, cols], w2w, w2s, t, z_w, z_s)
+                matmul(a_banks[2 * h + t // 2][:, t % 2, :], w2w, w2s, t, z_w, z_s)
 
-        gate = []
+        gate = new("gate", [P, PACK, S], F32)
         for t in range(PACK):
             sig = new("sig%d" % t, [P, S + 16], F32)
             nc.scalar.activation(sig[:, :S], b_banks[t][:], ACT.Tanh, scale=0.03125)
-            gate.append(new("gate%d" % t, [P, S], F32))
-            nc.scalar.activation(gate[t][:], sig[:].indirect(n4_t[:]), ACT.Copy)
+            nc.scalar.activation(gate[:, t, :], sig[:].indirect(n4_t[:]), ACT.Copy, scale=0.5, bias=0.5)
 
+        gated = [new("gated%d" % n, [P, 2, HALF], F32) for n in range(PACK)]
+        for n in range(PACK):
+            h, pair = divmod(n, 2)
+            nc.vector.tensor_tensor(
+                gated[n][:], a_banks[n][:], gate[:, 2 * pair : 2 * pair + 2, HALF * h : HALF * (h + 1)], ALU.mult
+            )
         a_half = [new("a_half%d" % t, [P, S], F32) for t in range(PACK)]
-        gated = [new("gated%d" % t, [P, S], F32) for t in range(PACK)]
         for t in range(PACK):
-            nc.scalar.activation(a_half[t][:], a_banks[t][:], ACT.Copy, scale=-0.5)
-            nc.vector.scalar_tensor_tensor(gated[t][:], gate[t][:], 1.0, a_half[t][:], ALU.add, ALU.mult)
+            for h in range(2):
+                nc.scalar.activation(
+                    a_half[t][:, HALF * h : HALF * (h + 1)], a_banks[2 * h + t // 2][:, t % 2, :], ACT.Copy, scale=-0.5
+                )
 
         out_rows = out_0.rearrange("(p t) j -> p t j", t=PACK)
         out_w = new("out_w", [P, S], U32)
         out_s = new("out_s", [P, S], U8)
-        for h in range(2):
-            cols = slice(HALF * h, HALF * (h + 1))
-            lcols = slice(HALF_COLS * h, HALF_COLS * (h + 1))
-            res = new("res%d" % h, [P, PACK, HALF], F32)
+        for start, width in ((0, 256), (256, 128), (384, 128)):
+            cols = slice(start, start + width)
+            h, inner = divmod(start, HALF)
+            res = new("res%d" % start, [P, PACK, width], F32)
             for t in range(PACK):
-                looked_up = a_half[t][:].indirect(n3_t[:, lcols])
-                if t == 0:
-                    nc.vector.tensor_tensor(res[:, t, :], looked_up, gated[t][:, cols], ALU.subtract)
+                looked_up = a_half[t][:].indirect(n3_t[:, start // 16 : (start + width) // 16])
+                own = gated[2 * h + t // 2][:, t % 2, inner : inner + width]
+                if t < (2 if start == 0 else 1):
+                    nc.vector.tensor_tensor(res[:, t, :], looked_up, own, ALU.add)
                 else:
-                    far = new("far%d%d" % (h, t), [P, HALF], F32)
+                    far = new("far%d_%d" % (start, t), [P, width], F32)
                     nc.scalar.activation(far[:], looked_up, ACT.Copy)
-                    nc.vector.tensor_tensor(res[:, t, :], far[:], gated[t][:, cols], ALU.subtract)
+                    nc.vector.tensor_tensor(res[:, t, :], far[:], own, ALU.add)
             nc.sync.dma_start(out=out_rows[:, :, cols], in_=res[:])
-            res_bf = new("res_bf%d" % h, [P, HALF * PACK], BF16)
+            res_bf = new("res_bf%d" % start, [P, width * PACK], BF16)
             nc.vector.tensor_copy(woven(res_bf), by_pairs(res[:]))
             nc.vector.quantize_mx(out=out_w[:, cols].bitcast(FP8X4), scales=out_s[:, cols], in_=res_bf[:])
             nc.sync.dma_start(out=words_of(out_1)[:, cols], in_=out_w[:, cols].bitcast(I32))
         for q in range(4):
-            nc.sync.dma_start(out=out_2[0, 4 * q : 4 * q + 4, :].bitcast(I32), in_=out_s[32 * q : 32 * q + 4, :].bitcast(I32))
+            queue = nc.scalar if q < 2 else nc.sync
+            queue.dma_start(out=out_2[0, 4 * q : 4 * q + 4, :].bitcast(I32), in_=out_s[32 * q : 32 * q + 4, :].bitcast(I32))

@@ -89,18 +89,18 @@ def tile_picked_cdjoingatebrange_none_po_kernel(
         nc.gpsimd.memset(ds_plane[:].bitcast(I32), 0)
 
         offs_t = load_list("offs_t", offs)
+        w1w_raw = load_words("w1w_raw", w1_words, S)
         load_plane(xs_table, x_scales, range(4))
         two_t = load_list("two_t", two)
         xw_table = load_words("xw_table", x_words, TABLE)
-        w1w_raw = load_words("w1w_raw", w1_words, S)
         load_plane(w1s_raw, w1_scales, range(4))
         gain = new("gain", [P, PACK], F32)
         nc.sync.dma_start(out=gain[:], in_=gn.rearrange("(p t) o -> p (t o)", t=PACK))
+        n1_t = load_list("n1_t", n1)
         dw_table = load_words("dw_table", d_words, TABLE)
         k1_t = load_list("k1_t", k1)
         for r in range(2):
             nc.sync.dma_start(out=ds_table[r:P:16, :].bitcast(I32), in_=d_scales[0, r:16:2, :].bitcast(I32))
-        n1_t = load_list("n1_t", n1)
         n2_t = load_list("n2_t", n2)
         w2w_raw = load_words("w2w_raw", w2_words, S)
         load_plane(w2s_raw, w2_scales, range(4))
@@ -123,22 +123,21 @@ def tile_picked_cdjoingatebrange_none_po_kernel(
         nc.scalar.copy(dealt_words(w1w), deal_words(w1w_raw))
         nc.vector.tensor_copy(dealt_scales(w1s), deal_scales(w1s_raw))
 
-        twice = new("twice", [P, PACK], F32)
-        sign = new("sign", [P, PACK], BF16)
         size = new("size", [P, PACK], F32)
-        nc.vector.tensor_scalar(twice[:], gain[:], 0.0, 2.0, ALU.is_ge, ALU.mult)
+        sign = new("sign", [P, HALF, PACK], BF16)
         nc.scalar.activation(size[:], gain[:], ACT.Abs)
-        nc.vector.tensor_scalar(sign[:], twice[:], -1.0, None, ALU.add)
+        nc.scalar.activation(sign[:], gain[:].unsqueeze(1).to_broadcast([P, HALF, PACK]), ACT.Sign)
 
-        y = []
+        y, pa, y_banks = [], [], []
         for t in range(PACK):
             bank = ps.tile([P, S], F32, name="ya%d" % t, tag="ya%d" % t)
             matmul(bank[:], w1w, w1s, t, xq_w, xq_s)
+            y_banks.append(bank)
             y.append(new("y%d" % t, [P, 2 * S], F32))
             nc.scalar.activation(y[t][:, :S], bank[:], ACT.Copy, scale=size[:, t : t + 1])
+            pa.append(new("pa%d" % t, [P, S], F32))
+            nc.scalar.activation(pa[t][:], y[t][:].indirect(n1_t[:]), ACT.Copy)
 
-        w2w = new("w2w", [P, S], U32)
-        w2s = new("w2s", [P, S], U8)
 
         x2_s = new("x2_s", [P, S], U8)
         x2_w = new("x2_w", [P, S], U32, over="w1s_raw")
@@ -160,37 +159,50 @@ def tile_picked_cdjoingatebrange_none_po_kernel(
             b_banks.append(ps.tile([P, S], F32, name="b%d" % t))
             matmul(b_banks[t][:], dw, ds_plane, t, x2_w, x2_s)
 
-        top = new("top", [P, PACK, S], F32)
-        low = new("low", [P, PACK, S], F32)
-        for t in range(PACK):
-            pa = new("pa%d" % t, [P, S], F32)
-            pbh = new("pbh%d" % t, [P, S], F32)
-            hi = new("hi%d" % t, [P, S], F32, over=["dw_table", "dq_w", "pa0", "pa1"][t])[:]
-            lo = new("lo%d" % t, [P, S], F32, over=["ds_table", "dq_s", "pbh0", "pbh1"][t])[:]
-            nc.scalar.activation(pa[:], y[t][:].indirect(n1_t[:]), ACT.Copy)
-            nc.scalar.activation(pbh[:], y[t][:].indirect(n2_t[:]), ACT.Copy, scale=0.5)
-            nc.vector.tensor_tensor(hi, y[t][:, :S], pa[:], ALU.max)
-            nc.vector.tensor_tensor(lo, y[t][:, :S], pa[:], ALU.min)
-            nc.vector.scalar_tensor_tensor(top[:, t, :], pbh[:], 2.0, hi, ALU.mult, ALU.max)
-            nc.vector.scalar_tensor_tensor(low[:, t, :], lo, 0.5, pbh[:], ALU.mult, ALU.min)
-
-        nc.vector.tensor_copy(dealt_words(w2w), deal_words(w2w_raw))
-        nc.vector.tensor_copy(dealt_scales(w2s), deal_scales(w2s_raw))
+        top = new("top", [P, 2, PACK, HALF], F32)
+        low = new("low", [P, 2, PACK, HALF], F32)
         a_banks = [ps.tile([P, 2, HALF], F32, name="a%d" % n, tag="ya%d" % n) for n in range(PACK)]
-        for h in range(2):
-            cols = slice(HALF * h, HALF * (h + 1))
+
+        def halves(ap):
+            return ap.rearrange("p (h c) -> p h c", h=2)
+
+        def second_product(h):
             z_abs = new("z_abs%d" % h, [P, HALF * PACK], BF16)
             z = new("z%d" % h, [P, HALF * PACK], BF16)
             z_w = new("z_w%d" % h, [P, HALF], U32)
             z_s = new("z_s%d" % h, [P, HALF], U8)
-            nc.vector.tensor_tensor(woven(z_abs), by_pairs(top[:, :, cols]), by_pairs(low[:, :, cols]), ALU.subtract)
-            nc.vector.tensor_tensor(
-                z[:].rearrange("p (c t) -> p c t", t=PACK), z_abs[:].rearrange("p (c t) -> p c t", t=PACK),
-                sign[:].unsqueeze(1).to_broadcast([P, HALF, PACK]), ALU.mult,
-            )
+            nc.vector.tensor_tensor(woven(z_abs), by_pairs(top[:, h]), by_pairs(low[:, h]), ALU.subtract)
+            nc.vector.tensor_tensor(z[:], z_abs[:], sign[:].rearrange("p c t -> p (c t)"), ALU.mult)
             nc.vector.quantize_mx(out=z_w[:].bitcast(FP8X4), scales=z_s[:], in_=z[:])
             for t in range(PACK):
                 matmul(a_banks[2 * h + t // 2][:, t % 2, :], w2w, w2s, t, z_w, z_s)
+
+        his, los = [], []
+        for t in range(PACK):
+            pair = new("pair%d" % t, [P, 2, S], F32, over=["dw_table", "dq_w", "pa0", "pa1"][t])
+            his.append(pair[:, 0, :])
+            los.append(pair[:, 1, :])
+            nc.vector.scalar_tensor_tensor(his[t], y_banks[t][:], size[:, t : t + 1], pa[t][:], ALU.mult, ALU.max)
+            nc.vector.scalar_tensor_tensor(los[t], y_banks[t][:], size[:, t : t + 1], pa[t][:], ALU.mult, ALU.min)
+        w2w = new("w2w", [P, S], U32, over="dq_s")
+        w2s = new("w2s", [P, S], U8, over="ds_dealt")
+        nc.gpsimd.tensor_copy(dealt_words(w2w), deal_words(w2w_raw))
+        nc.gpsimd.tensor_copy(dealt_scales(w2s), deal_scales(w2s_raw))
+        for t in range(PACK):
+            pbh = new("pbh%d" % t, [P, S], F32)
+            hi, lo = his[t], los[t]
+            if t < PACK - 1:
+                nc.scalar.activation(pbh[:], y[t][:].indirect(n2_t[:]), ACT.Copy, scale=0.5)
+                nc.vector.scalar_tensor_tensor(top[:, :, t, :], halves(pbh[:]), 2.0, halves(hi), ALU.mult, ALU.max)
+                nc.vector.scalar_tensor_tensor(low[:, :, t, :], halves(lo), 0.5, halves(pbh[:]), ALU.mult, ALU.min)
+            else:
+                for h in range(2):
+                    cols = slice(HALF * h, HALF * (h + 1))
+                    lcols = slice(HALF_COLS * h, HALF_COLS * (h + 1))
+                    nc.scalar.activation(pbh[:, cols], y[t][:].indirect(n2_t[:, lcols]), ACT.Copy, scale=0.5)
+                    nc.vector.scalar_tensor_tensor(top[:, h, t, :], pbh[:, cols], 2.0, hi[:, cols], ALU.mult, ALU.max)
+                    nc.vector.scalar_tensor_tensor(low[:, h, t, :], lo[:, cols], 0.5, pbh[:, cols], ALU.mult, ALU.min)
+                    second_product(h)
 
         gate = new("gate", [P, PACK, S], F32)
         for t in range(PACK):
@@ -199,7 +211,7 @@ def tile_picked_cdjoingatebrange_none_po_kernel(
             nc.scalar.activation(gate[:, t, :], sig[:].indirect(n4_t[:]), ACT.Copy, scale=0.5, bias=0.5)
 
         gated = [new("gated%d" % n, [P, 2, HALF], F32) for n in range(PACK)]
-        for n in range(PACK):
+        for n in (0, 2, 1, 3):
             h, pair = divmod(n, 2)
             nc.vector.tensor_tensor(
                 gated[n][:], a_banks[n][:], gate[:, 2 * pair : 2 * pair + 2, HALF * h : HALF * (h + 1)], ALU.mult

@@ -16,9 +16,11 @@ P = 128
 PACK = 4
 TABLE = 2048
 S = 512
-HALF = 256
-LIST_COLS = S // 16
-HALF_COLS = HALF // 16
+HALF = S // 2
+PER_COL = 16
+
+OUT_RUNS = ((0, 256), (256, 128), (384, 128))
+FUSED_TILES = (2, 2, 1)
 
 FLOPS = 3 * 2 * 512 * 512 * 512
 
@@ -27,28 +29,27 @@ def words_of(dram):
     return dram[0].rearrange("p n t -> p (n t)").bitcast(I32)
 
 
-def deal_words(tile):
-    return tile[:].rearrange("p (b i t) -> p b t i", i=4, t=PACK)
+def entries(list_tile, start, count):
+    return list_tile[:, start // PER_COL : (start + count) // PER_COL]
 
 
-def dealt_words(tile):
-    return tile[:].rearrange("p (t b i) -> p b t i", i=4, t=PACK)
+def deal(copy, dealt, plain, run):
+    copy(
+        dealt[:].rearrange("p (t b i) -> p b t i", i=run, t=PACK),
+        plain[:].rearrange("p (b i t) -> p b t i", i=run, t=PACK),
+    )
 
 
-def deal_scales(tile):
-    return tile[:].rearrange("p (b i t) -> p b t i", i=16, t=PACK)
-
-
-def dealt_scales(tile):
-    return tile[:].rearrange("p (t b i) -> p b t i", i=16, t=PACK)
-
-
-def by_pairs(tile):
-    return tile.rearrange("p t (c i) -> p c t i", i=2)
+def by_pairs(tiles):
+    return tiles.rearrange("p t (c i) -> p c t i", i=2)
 
 
 def woven(tile):
     return tile[:].rearrange("p (c i t) -> p c t i", i=2, t=PACK)
+
+
+def halves(ap):
+    return ap.rearrange("p (h c) -> p h c", h=2)
 
 
 def tile_picked_cdjoingatebrange_none_po_kernel(
@@ -64,7 +65,7 @@ def tile_picked_cdjoingatebrange_none_po_kernel(
             return sb.tile(shape, dtype, name=name, tag=over or name, align_bytes=64)
 
         def load_list(name, dram):
-            tile = new(name, [P, LIST_COLS], U16)
+            tile = new(name, [P, S // PER_COL], U16)
             nc.sync.dma_start(tile[:], dram)
             return tile
 
@@ -73,27 +74,34 @@ def tile_picked_cdjoingatebrange_none_po_kernel(
             nc.sync.dma_start(out=tile[:].bitcast(I32), in_=words_of(dram))
             return tile
 
-        def load_plane(tile, dram, quadrants):
-            for q in quadrants:
+        def load_plane(tile, dram):
+            for q in range(4):
                 nc.sync.dma_start(out=tile[32 * q : 32 * q + 4, :].bitcast(I32), in_=dram[0, 4 * q : 4 * q + 4, :].bitcast(I32))
 
+        def matmul(out, lhs_words, lhs_plane, t, rhs_words, rhs_plane):
+            rows = slice(P * t, P * (t + 1))
+            nc.tensor.matmul_mx(
+                out=out, lhsT=lhs_words[:, rows].bitcast(FP8X4), lhsT_scale=lhs_plane[:, rows],
+                rhs=rhs_words.bitcast(FP8X4), rhs_scale=rhs_plane, start=True, stop=True,
+            )
+
         xs_table = new("xs_table", [P, TABLE], U8)
-        w1s_raw = new("w1s_raw", [P, S], U8)
+        w1s_plain = new("w1s_plain", [P, S], U8)
         ds_table = new("ds_table", [P, TABLE], U8)
-        w2s_raw = new("w2s_raw", [P, S], U8)
+        w2s_plain = new("w2s_plain", [P, S], U8)
         ds_plane = new("ds_plane", [P, S], U8)
         nc.gpsimd.memset(xs_table[:].bitcast(I32), 0)
-        nc.gpsimd.memset(w1s_raw[:].bitcast(I32), 0)
+        nc.gpsimd.memset(w1s_plain[:].bitcast(I32), 0)
         nc.vector.memset(ds_table[:].bitcast(I32), 0)
-        nc.gpsimd.memset(w2s_raw[:].bitcast(I32), 0)
+        nc.gpsimd.memset(w2s_plain[:].bitcast(I32), 0)
         nc.gpsimd.memset(ds_plane[:].bitcast(I32), 0)
 
         offs_t = load_list("offs_t", offs)
-        w1w_raw = load_words("w1w_raw", w1_words, S)
-        load_plane(xs_table, x_scales, range(4))
+        w1w_plain = load_words("w1w_plain", w1_words, S)
+        load_plane(xs_table, x_scales)
         two_t = load_list("two_t", two)
         xw_table = load_words("xw_table", x_words, TABLE)
-        load_plane(w1s_raw, w1_scales, range(4))
+        load_plane(w1s_plain, w1_scales)
         gain = new("gain", [P, PACK], F32)
         nc.sync.dma_start(out=gain[:], in_=gn.rearrange("(p t) o -> p (t o)", t=PACK))
         n1_t = load_list("n1_t", n1)
@@ -102,17 +110,10 @@ def tile_picked_cdjoingatebrange_none_po_kernel(
         for r in range(2):
             nc.sync.dma_start(out=ds_table[r:P:16, :].bitcast(I32), in_=d_scales[0, r:16:2, :].bitcast(I32))
         n2_t = load_list("n2_t", n2)
-        w2w_raw = load_words("w2w_raw", w2_words, S)
-        load_plane(w2s_raw, w2_scales, range(4))
+        w2w_plain = load_words("w2w_plain", w2_words, S)
+        load_plane(w2s_plain, w2_scales)
         n4_t = load_list("n4_t", n4)
         n3_t = load_list("n3_t", n3)
-
-        def matmul(out, lhs_w, lhs_s, t, rhs_w, rhs_s):
-            rows = slice(P * t, P * (t + 1))
-            nc.tensor.matmul_mx(
-                out=out, lhsT=lhs_w[:, rows].bitcast(FP8X4), lhsT_scale=lhs_s[:, rows],
-                rhs=rhs_w[:].bitcast(FP8X4), rhs_scale=rhs_s[:], start=True, stop=True,
-            )
 
         xq_s = new("xq_s", [P, S], U8)
         xq_w = new("xq_w", [P, S], U32)
@@ -120,51 +121,52 @@ def tile_picked_cdjoingatebrange_none_po_kernel(
         w1s = new("w1s", [P, S], U8)
         nc.vector.tensor_copy(xq_s[:], xs_table[:].indirect(offs_t[:]))
         nc.vector.tensor_copy(xq_w[:], xw_table[:].indirect(offs_t[:]))
-        nc.scalar.copy(dealt_words(w1w), deal_words(w1w_raw))
-        nc.vector.tensor_copy(dealt_scales(w1s), deal_scales(w1s_raw))
+        deal(nc.scalar.copy, w1w, w1w_plain, 4)
+        deal(nc.gpsimd.tensor_copy, w1s, w1s_plain, 16)
 
         size = new("size", [P, PACK], F32)
         sign = new("sign", [P, HALF, PACK], BF16)
         nc.scalar.activation(size[:], gain[:], ACT.Abs)
         nc.scalar.activation(sign[:], gain[:].unsqueeze(1).to_broadcast([P, HALF, PACK]), ACT.Sign)
 
-        y, pa, y_banks = [], [], []
+        v, v_n1, y_banks = [], [], []
         for t in range(PACK):
-            bank = ps.tile([P, S], F32, name="ya%d" % t, tag="ya%d" % t)
-            matmul(bank[:], w1w, w1s, t, xq_w, xq_s)
-            y_banks.append(bank)
-            y.append(new("y%d" % t, [P, 2 * S], F32))
-            nc.scalar.activation(y[t][:, :S], bank[:], ACT.Copy, scale=size[:, t : t + 1])
-            pa.append(new("pa%d" % t, [P, S], F32))
-            nc.scalar.activation(pa[t][:], y[t][:].indirect(n1_t[:]), ACT.Copy)
+            y_banks.append(ps.tile([P, S], F32, name="y%d" % t, tag="ya%d" % t))
+            matmul(y_banks[t][:], w1w, w1s, t, xq_w[:], xq_s[:])
+            v.append(new("v%d" % t, [P, 2 * S], F32))
+            nc.scalar.activation(v[t][:, :S], y_banks[t][:], ACT.Copy, scale=size[:, t : t + 1])
+            v_n1.append(new("v_n1_%d" % t, [P, S], F32))
+            nc.scalar.activation(v_n1[t][:], v[t][:].indirect(n1_t[:]), ACT.Copy)
 
-
-        x2_s = new("x2_s", [P, S], U8)
-        x2_w = new("x2_w", [P, S], U32, over="w1s_raw")
+        x2_s = [new("x2_s0", [P, HALF], U8), new("x2_s1", [P, HALF], U8, over="w1s_plain")]
+        x2_w = new("x2_w", [P, S], U32)
         dq_s = new("dq_s", [P, S], U8)
         dq_w = new("dq_w", [P, S], U32)
         ds_dealt = new("ds_dealt", [P, S], U8)
         dw = new("dw", [P, S], U32)
-        nc.vector.tensor_copy(x2_s[:], xs_table[:].indirect(two_t[:]))
+        nc.vector.tensor_copy(x2_s[0][:], xs_table[:].indirect(entries(two_t, 0, HALF)))
         nc.vector.tensor_copy(x2_w[:], xw_table[:].indirect(two_t[:]))
+        nc.vector.tensor_copy(x2_s[1][:], xs_table[:].indirect(entries(two_t, HALF, HALF)))
         nc.vector.tensor_copy(dq_w[:], dw_table[:].indirect(k1_t[:]))
         nc.vector.tensor_copy(dq_s[:], ds_table[:].indirect(k1_t[:]))
-        nc.vector.tensor_copy(dealt_words(dw), deal_words(dq_w))
-        nc.vector.tensor_copy(dealt_scales(ds_dealt), deal_scales(dq_s))
+        deal(nc.vector.tensor_copy, dw, dq_w, 4)
+        deal(nc.vector.tensor_copy, ds_dealt, dq_s, 16)
         for r in range(4):
-            src = 16 * (r // 2) + r % 2
-            nc.sync.dma_start(out=ds_plane[r:P:32, :].bitcast(I32), in_=ds_dealt[src:P:32, :].bitcast(I32))
+            gathered_on = 16 * (r // 2) + r % 2
+            nc.sync.dma_start(out=ds_plane[r:P:32, :].bitcast(I32), in_=ds_dealt[gathered_on:P:32, :].bitcast(I32))
         b_banks = []
         for t in range(PACK):
             b_banks.append(ps.tile([P, S], F32, name="b%d" % t))
-            matmul(b_banks[t][:], dw, ds_plane, t, x2_w, x2_s)
+            for h in range(2):
+                cols = slice(HALF * h, HALF * (h + 1))
+                matmul(b_banks[t][:, cols], dw, ds_plane, t, x2_w[:, cols], x2_s[h][:])
 
         top = new("top", [P, 2, PACK, HALF], F32)
         low = new("low", [P, 2, PACK, HALF], F32)
         a_banks = [ps.tile([P, 2, HALF], F32, name="a%d" % n, tag="ya%d" % n) for n in range(PACK)]
 
-        def halves(ap):
-            return ap.rearrange("p (h c) -> p h c", h=2)
+        def a_of(t, h):
+            return a_banks[2 * h + t // 2][:, t % 2, :]
 
         def second_product(h):
             z_abs = new("z_abs%d" % h, [P, HALF * PACK], BF16)
@@ -175,65 +177,60 @@ def tile_picked_cdjoingatebrange_none_po_kernel(
             nc.vector.tensor_tensor(z[:], z_abs[:], sign[:].rearrange("p c t -> p (c t)"), ALU.mult)
             nc.vector.quantize_mx(out=z_w[:].bitcast(FP8X4), scales=z_s[:], in_=z[:])
             for t in range(PACK):
-                matmul(a_banks[2 * h + t // 2][:, t % 2, :], w2w, w2s, t, z_w, z_s)
+                matmul(a_of(t, h), w2w, w2s, t, z_w[:], z_s[:])
 
-        his, los = [], []
+        larger, smaller = [], []
         for t in range(PACK):
-            pair = new("pair%d" % t, [P, 2, S], F32, over=["dw_table", "dq_w", "pa0", "pa1"][t])
-            his.append(pair[:, 0, :])
-            los.append(pair[:, 1, :])
-            nc.vector.scalar_tensor_tensor(his[t], y_banks[t][:], size[:, t : t + 1], pa[t][:], ALU.mult, ALU.max)
-            nc.vector.scalar_tensor_tensor(los[t], y_banks[t][:], size[:, t : t + 1], pa[t][:], ALU.mult, ALU.min)
+            pair = new("pair%d" % t, [P, 2, S], F32, over=["dw_table", "dq_w", "v_n1_0", "v_n1_1"][t])
+            larger.append(pair[:, 0, :])
+            smaller.append(pair[:, 1, :])
+            nc.vector.scalar_tensor_tensor(larger[t], y_banks[t][:], size[:, t : t + 1], v_n1[t][:], ALU.mult, ALU.max)
+            nc.vector.scalar_tensor_tensor(smaller[t], y_banks[t][:], size[:, t : t + 1], v_n1[t][:], ALU.mult, ALU.min)
         w2w = new("w2w", [P, S], U32, over="dq_s")
         w2s = new("w2s", [P, S], U8, over="ds_dealt")
-        nc.gpsimd.tensor_copy(dealt_words(w2w), deal_words(w2w_raw))
-        nc.gpsimd.tensor_copy(dealt_scales(w2s), deal_scales(w2s_raw))
+        deal(nc.gpsimd.tensor_copy, w2w, w2w_plain, 4)
+        deal(nc.gpsimd.tensor_copy, w2s, w2s_plain, 16)
         for t in range(PACK):
-            pbh = new("pbh%d" % t, [P, S], F32)
-            hi, lo = his[t], los[t]
+            half_n2 = new("half_n2_%d" % t, [P, S], F32)
             if t < PACK - 1:
-                nc.scalar.activation(pbh[:], y[t][:].indirect(n2_t[:]), ACT.Copy, scale=0.5)
-                nc.vector.scalar_tensor_tensor(top[:, :, t, :], halves(pbh[:]), 2.0, halves(hi), ALU.mult, ALU.max)
-                nc.vector.scalar_tensor_tensor(low[:, :, t, :], halves(lo), 0.5, halves(pbh[:]), ALU.mult, ALU.min)
+                nc.scalar.activation(half_n2[:], v[t][:].indirect(n2_t[:]), ACT.Copy, scale=0.5)
+                nc.vector.scalar_tensor_tensor(top[:, :, t, :], halves(half_n2[:]), 2.0, halves(larger[t]), ALU.mult, ALU.max)
+                nc.vector.scalar_tensor_tensor(low[:, :, t, :], halves(smaller[t]), 0.5, halves(half_n2[:]), ALU.mult, ALU.min)
             else:
                 for h in range(2):
                     cols = slice(HALF * h, HALF * (h + 1))
-                    lcols = slice(HALF_COLS * h, HALF_COLS * (h + 1))
-                    nc.scalar.activation(pbh[:, cols], y[t][:].indirect(n2_t[:, lcols]), ACT.Copy, scale=0.5)
-                    nc.vector.scalar_tensor_tensor(top[:, h, t, :], pbh[:, cols], 2.0, hi[:, cols], ALU.mult, ALU.max)
-                    nc.vector.scalar_tensor_tensor(low[:, h, t, :], lo[:, cols], 0.5, pbh[:, cols], ALU.mult, ALU.min)
+                    nc.scalar.activation(half_n2[:, cols], v[t][:].indirect(entries(n2_t, HALF * h, HALF)), ACT.Copy, scale=0.5)
+                    nc.vector.scalar_tensor_tensor(top[:, h, t, :], half_n2[:, cols], 2.0, larger[t][:, cols], ALU.mult, ALU.max)
+                    nc.vector.scalar_tensor_tensor(low[:, h, t, :], smaller[t][:, cols], 0.5, half_n2[:, cols], ALU.mult, ALU.min)
                     second_product(h)
 
         gate = new("gate", [P, PACK, S], F32)
         for t in range(PACK):
-            sig = new("sig%d" % t, [P, S + 16], F32)
-            nc.scalar.activation(sig[:, :S], b_banks[t][:], ACT.Tanh, scale=0.03125)
-            nc.scalar.activation(gate[:, t, :], sig[:].indirect(n4_t[:]), ACT.Copy, scale=0.5, bias=0.5)
+            tanh_b = new("tanh_b%d" % t, [P, S + PER_COL], F32)
+            nc.scalar.activation(tanh_b[:, :S], b_banks[t][:], ACT.Tanh, scale=0.0625 / 2)
+            nc.scalar.activation(gate[:, t, :], tanh_b[:].indirect(n4_t[:]), ACT.Copy, scale=0.5, bias=0.5)
 
         gated = [new("gated%d" % n, [P, 2, HALF], F32) for n in range(PACK)]
-        for n in (0, 2, 1, 3):
-            h, pair = divmod(n, 2)
-            nc.vector.tensor_tensor(
-                gated[n][:], a_banks[n][:], gate[:, 2 * pair : 2 * pair + 2, HALF * h : HALF * (h + 1)], ALU.mult
-            )
+        for first in range(0, PACK, 2):
+            for h in range(2):
+                n = 2 * h + first // 2
+                nc.vector.tensor_tensor(gated[n][:], a_banks[n][:], gate[:, first : first + 2, HALF * h : HALF * (h + 1)], ALU.mult)
         a_half = [new("a_half%d" % t, [P, S], F32) for t in range(PACK)]
         for t in range(PACK):
             for h in range(2):
-                nc.scalar.activation(
-                    a_half[t][:, HALF * h : HALF * (h + 1)], a_banks[2 * h + t // 2][:, t % 2, :], ACT.Copy, scale=-0.5
-                )
+                nc.scalar.activation(a_half[t][:, HALF * h : HALF * (h + 1)], a_of(t, h), ACT.Copy, scale=-0.5)
 
         out_rows = out_0.rearrange("(p t) j -> p t j", t=PACK)
         out_w = new("out_w", [P, S], U32)
         out_s = new("out_s", [P, S], U8)
-        for start, width in ((0, 256), (256, 128), (384, 128)):
+        for (start, width), fused in zip(OUT_RUNS, FUSED_TILES):
             cols = slice(start, start + width)
             h, inner = divmod(start, HALF)
             res = new("res%d" % start, [P, PACK, width], F32)
             for t in range(PACK):
-                looked_up = a_half[t][:].indirect(n3_t[:, start // 16 : (start + width) // 16])
+                looked_up = a_half[t][:].indirect(entries(n3_t, start, width))
                 own = gated[2 * h + t // 2][:, t % 2, inner : inner + width]
-                if t < (2 if start == 0 else 1):
+                if t < fused:
                     nc.vector.tensor_tensor(res[:, t, :], looked_up, own, ALU.add)
                 else:
                     far = new("far%d_%d" % (start, t), [P, width], F32)

from contextlib import ExitStack

import concourse.mybir as mybir

F32 = mybir.dt.float32
BF16 = mybir.dt.bfloat16
I32 = mybir.dt.int32
U32 = mybir.dt.uint32
U16 = mybir.dt.uint16
U8 = mybir.dt.uint8
FP8X4 = mybir.dt.float8_e4m3fn_x4
ALU = mybir.AluOpType
ACT = mybir.ActivationFunctionType

P = 128
PACK = 4
TABLE = 2048
S = 512
HALF = S // 2
PER_COL = 16

OUT_RUNS = ((0, 256), (256, 128), (384, 128))
FUSED_TILES = (2, 2, 1)

FLOPS = 3 * 2 * 512 * 512 * 512


def words_of(dram):
    return dram[0].rearrange("p n t -> p (n t)").bitcast(I32)


def entries(list_tile, start, count):
    return list_tile[:, start // PER_COL : (start + count) // PER_COL]


def deal(copy, dealt, plain, run):
    copy(
        dealt[:].rearrange("p (t b i) -> p b t i", i=run, t=PACK),
        plain[:].rearrange("p (b i t) -> p b t i", i=run, t=PACK),
    )


def by_pairs(tiles):
    return tiles.rearrange("p t (c i) -> p c t i", i=2)


def woven(tile):
    return tile[:].rearrange("p (c i t) -> p c t i", i=2, t=PACK)


def halves(ap):
    return ap.rearrange("p (h c) -> p h c", h=2)


def tile_picked_cdjoingatebrange_none_po_kernel(
    tc, x_words, x_scales, w1_words, w1_scales, gn, w2_words, w2_scales, d_words, d_scales,
    offs, n1, n2, two, k1, n3, n4, out_0, out_1, out_2,
):
    nc = tc.nc
    with ExitStack() as ctx:
        sb = ctx.enter_context(tc.tile_pool(name="sb", bufs=1))
        ps = ctx.enter_context(tc.psum_pool(name="ps", bufs=1))

        def new(name, shape, dtype, over=None):
            return sb.tile(shape, dtype, name=name, tag=over or name, align_bytes=64)

        def load_list(name, dram):
            tile = new(name, [P, S // PER_COL], U16)
            nc.sync.dma_start(tile[:], dram)
            return tile

        def load_words(name, dram, width):
            tile = new(name, [P, width], U32)
            nc.sync.dma_start(out=tile[:].bitcast(I32), in_=words_of(dram))
            return tile

        def load_plane(tile, dram):
            for q in range(4):
                nc.sync.dma_start(out=tile[32 * q : 32 * q + 4, :].bitcast(I32), in_=dram[0, 4 * q : 4 * q + 4, :].bitcast(I32))

        def matmul(out, lhs_words, lhs_plane, t, rhs_words, rhs_plane):
            rows = slice(P * t, P * (t + 1))
            nc.tensor.matmul_mx(
                out=out, lhsT=lhs_words[:, rows].bitcast(FP8X4), lhsT_scale=lhs_plane[:, rows],
                rhs=rhs_words.bitcast(FP8X4), rhs_scale=rhs_plane, start=True, stop=True,
            )

        xs_table = new("xs_table", [P, TABLE], U8)
        w1s_plain = new("w1s_plain", [P, S], U8)
        ds_table = new("ds_table", [P, TABLE], U8)
        w2s_plain = new("w2s_plain", [P, S], U8)
        ds_plane = new("ds_plane", [P, S], U8)
        nc.gpsimd.memset(xs_table[:].bitcast(I32), 0)
        nc.gpsimd.memset(w1s_plain[:].bitcast(I32), 0)
        nc.vector.memset(ds_table[:].bitcast(I32), 0)
        nc.gpsimd.memset(w2s_plain[:].bitcast(I32), 0)
        nc.gpsimd.memset(ds_plane[:].bitcast(I32), 0)

        offs_t = load_list("offs_t", offs)
        w1w_plain = load_words("w1w_plain", w1_words, S)
        load_plane(xs_table, x_scales)
        two_t = load_list("two_t", two)
        xw_table = load_words("xw_table", x_words, TABLE)
        load_plane(w1s_plain, w1_scales)
        gain = new("gain", [P, PACK], F32)
        nc.sync.dma_start(out=gain[:], in_=gn.rearrange("(p t) o -> p (t o)", t=PACK))
        n1_t = load_list("n1_t", n1)
        dw_table = load_words("dw_table", d_words, TABLE)
        k1_t = load_list("k1_t", k1)
        for r in range(2):
            nc.sync.dma_start(out=ds_table[r:P:16, :].bitcast(I32), in_=d_scales[0, r:16:2, :].bitcast(I32))
        n2_t = load_list("n2_t", n2)
        w2w_plain = load_words("w2w_plain", w2_words, S)
        load_plane(w2s_plain, w2_scales)
        n4_t = load_list("n4_t", n4)
        n3_t = load_list("n3_t", n3)

        xq_s = new("xq_s", [P, S], U8)
        xq_w = new("xq_w", [P, S], U32)
        w1w = new("w1w", [P, S], U32)
        w1s = new("w1s", [P, S], U8)
        nc.vector.tensor_copy(xq_s[:], xs_table[:].indirect(offs_t[:]))
        nc.vector.tensor_copy(xq_w[:], xw_table[:].indirect(offs_t[:]))
        deal(nc.scalar.copy, w1w, w1w_plain, 4)
        deal(nc.gpsimd.tensor_copy, w1s, w1s_plain, 16)

        size = new("size", [P, PACK], F32)
        sign = new("sign", [P, HALF, PACK], BF16)
        nc.scalar.activation(size[:], gain[:], ACT.Abs)
        nc.scalar.activation(sign[:], gain[:].unsqueeze(1).to_broadcast([P, HALF, PACK]), ACT.Sign)

        v, v_n1, y_banks = [], [], []
        for t in range(PACK):
            y_banks.append(ps.tile([P, S], F32, name="y%d" % t, tag="ya%d" % t))
            matmul(y_banks[t][:], w1w, w1s, t, xq_w[:], xq_s[:])
            v.append(new("v%d" % t, [P, 2 * S], F32))
            nc.scalar.activation(v[t][:, :S], y_banks[t][:], ACT.Copy, scale=size[:, t : t + 1])
            v_n1.append(new("v_n1_%d" % t, [P, S], F32))
            nc.scalar.activation(v_n1[t][:], v[t][:].indirect(n1_t[:]), ACT.Copy)

        x2_s = [new("x2_s0", [P, HALF], U8), new("x2_s1", [P, HALF], U8, over="w1s_plain")]
        x2_w = new("x2_w", [P, S], U32)
        dq_s = new("dq_s", [P, S], U8)
        dq_w = new("dq_w", [P, S], U32)
        ds_dealt = new("ds_dealt", [P, S], U8)
        dw = new("dw", [P, S], U32)
        nc.vector.tensor_copy(x2_s[0][:], xs_table[:].indirect(entries(two_t, 0, HALF)))
        nc.vector.tensor_copy(x2_w[:], xw_table[:].indirect(two_t[:]))
        nc.vector.tensor_copy(x2_s[1][:], xs_table[:].indirect(entries(two_t, HALF, HALF)))
        nc.vector.tensor_copy(dq_w[:], dw_table[:].indirect(k1_t[:]))
        nc.vector.tensor_copy(dq_s[:], ds_table[:].indirect(k1_t[:]))
        deal(nc.vector.tensor_copy, dw, dq_w, 4)
        deal(nc.vector.tensor_copy, ds_dealt, dq_s, 16)
        for r in range(4):
            gathered_on = 16 * (r // 2) + r % 2
            nc.sync.dma_start(out=ds_plane[r:P:32, :].bitcast(I32), in_=ds_dealt[gathered_on:P:32, :].bitcast(I32))
        b_banks = []
        for t in range(PACK):
            b_banks.append(ps.tile([P, S], F32, name="b%d" % t))
            for h in range(2):
                cols = slice(HALF * h, HALF * (h + 1))
                matmul(b_banks[t][:, cols], dw, ds_plane, t, x2_w[:, cols], x2_s[h][:])

        top = new("top", [P, 2, PACK, HALF], F32)
        low = new("low", [P, 2, PACK, HALF], F32)
        a_banks = [ps.tile([P, 2, HALF], F32, name="a%d" % n, tag="ya%d" % n) for n in range(PACK)]

        def a_of(t, h):
            return a_banks[2 * h + t // 2][:, t % 2, :]

        def second_product(h):
            z_abs = new("z_abs%d" % h, [P, HALF * PACK], BF16)
            z = new("z%d" % h, [P, HALF * PACK], BF16)
            z_w = new("z_w%d" % h, [P, HALF], U32)
            z_s = new("z_s%d" % h, [P, HALF], U8)
            nc.vector.tensor_tensor(woven(z_abs), by_pairs(top[:, h]), by_pairs(low[:, h]), ALU.subtract)
            nc.vector.tensor_tensor(z[:], z_abs[:], sign[:].rearrange("p c t -> p (c t)"), ALU.mult)
            nc.vector.quantize_mx(out=z_w[:].bitcast(FP8X4), scales=z_s[:], in_=z[:])
            for t in range(PACK):
                matmul(a_of(t, h), w2w, w2s, t, z_w[:], z_s[:])

        larger, smaller = [], []
        for t in range(PACK):
            pair = new("pair%d" % t, [P, 2, S], F32, over=["dw_table", "dq_w", "v_n1_0", "v_n1_1"][t])
            larger.append(pair[:, 0, :])
            smaller.append(pair[:, 1, :])
            nc.vector.scalar_tensor_tensor(larger[t], y_banks[t][:], size[:, t : t + 1], v_n1[t][:], ALU.mult, ALU.max)
            nc.vector.scalar_tensor_tensor(smaller[t], y_banks[t][:], size[:, t : t + 1], v_n1[t][:], ALU.mult, ALU.min)
        w2w = new("w2w", [P, S], U32, over="dq_s")
        w2s = new("w2s", [P, S], U8, over="ds_dealt")
        deal(nc.gpsimd.tensor_copy, w2w, w2w_plain, 4)
        deal(nc.gpsimd.tensor_copy, w2s, w2s_plain, 16)
        for t in range(PACK):
            half_n2 = new("half_n2_%d" % t, [P, S], F32)
            if t < PACK - 1:
                nc.scalar.activation(half_n2[:], v[t][:].indirect(n2_t[:]), ACT.Copy, scale=0.5)
                nc.vector.scalar_tensor_tensor(top[:, :, t, :], halves(half_n2[:]), 2.0, halves(larger[t]), ALU.mult, ALU.max)
                nc.vector.scalar_tensor_tensor(low[:, :, t, :], halves(smaller[t]), 0.5, halves(half_n2[:]), ALU.mult, ALU.min)
            else:
                for h in range(2):
                    cols = slice(HALF * h, HALF * (h + 1))
                    nc.scalar.activation(half_n2[:, cols], v[t][:].indirect(entries(n2_t, HALF * h, HALF)), ACT.Copy, scale=0.5)
                    nc.vector.scalar_tensor_tensor(top[:, h, t, :], half_n2[:, cols], 2.0, larger[t][:, cols], ALU.mult, ALU.max)
                    nc.vector.scalar_tensor_tensor(low[:, h, t, :], smaller[t][:, cols], 0.5, half_n2[:, cols], ALU.mult, ALU.min)
                    second_product(h)

        gate = new("gate", [P, PACK, S], F32)
        for t in range(PACK):
            tanh_b = new("tanh_b%d" % t, [P, S + PER_COL], F32)
            nc.scalar.activation(tanh_b[:, :S], b_banks[t][:], ACT.Tanh, scale=0.0625 / 2)
            nc.scalar.activation(gate[:, t, :], tanh_b[:].indirect(n4_t[:]), ACT.Copy, scale=0.5, bias=0.5)

        gated = [new("gated%d" % n, [P, 2, HALF], F32) for n in range(PACK)]
        for first in range(0, PACK, 2):
            for h in range(2):
                n = 2 * h + first // 2
                nc.vector.tensor_tensor(gated[n][:], a_banks[n][:], gate[:, first : first + 2, HALF * h : HALF * (h + 1)], ALU.mult)
        a_half = [new("a_half%d" % t, [P, S], F32) for t in range(PACK)]
        for t in range(PACK):
            for h in range(2):
                nc.scalar.activation(a_half[t][:, HALF * h : HALF * (h + 1)], a_of(t, h), ACT.Copy, scale=-0.5)

        out_rows = out_0.rearrange("(p t) j -> p t j", t=PACK)
        out_w = new("out_w", [P, S], U32)
        out_s = new("out_s", [P, S], U8)
        for (start, width), fused in zip(OUT_RUNS, FUSED_TILES):
            cols = slice(start, start + width)
            h, inner = divmod(start, HALF)
            res = new("res%d" % start, [P, PACK, width], F32)
            for t in range(PACK):
                looked_up = a_half[t][:].indirect(entries(n3_t, start, width))
                own = gated[2 * h + t // 2][:, t % 2, inner : inner + width]
                if t < fused:
                    nc.vector.tensor_tensor(res[:, t, :], looked_up, own, ALU.add)
                else:
                    far = new("far%d_%d" % (start, t), [P, width], F32)
                    nc.scalar.activation(far[:], looked_up, ACT.Copy)
                    nc.vector.tensor_tensor(res[:, t, :], far[:], own, ALU.add)
            nc.sync.dma_start(out=out_rows[:, :, cols], in_=res[:])
            res_bf = new("res_bf%d" % start, [P, width * PACK], BF16)
            nc.vector.tensor_copy(woven(res_bf), by_pairs(res[:]))
            nc.vector.quantize_mx(out=out_w[:, cols].bitcast(FP8X4), scales=out_s[:, cols], in_=res_bf[:])
            nc.sync.dma_start(out=words_of(out_1)[:, cols], in_=out_w[:, cols].bitcast(I32))
        for q in range(4):
            queue = nc.scalar if q < 2 else nc.sync
            queue.dma_start(out=out_2[0, 4 * q : 4 * q + 4, :].bitcast(I32), in_=out_s[32 * q : 32 * q + 4, :].bitcast(I32))
